import numpy as np
import ml_dtypes


def mxq(x, axis, fmt="e4m3"):
    dtype, down = {"e4m3": (ml_dtypes.float8_e4m3fn, 7), "e5m2": (ml_dtypes.float8_e5m2, 14)}[fmt]
    v = np.moveaxis(np.asarray(x, np.float32).astype(ml_dtypes.bfloat16).astype(np.float64), axis, -1)
    blocks = v.reshape(v.shape[:-1] + (-1, 32))
    amax = np.abs(blocks).max(-1, keepdims=True)
    byte = np.maximum(np.where(amax > 0, np.frexp(amax)[1] - 1 + 127, 0) - down, 1)
    scale = np.exp2(byte - 127.0)
    codes = (blocks / scale).astype(np.float32).astype(dtype).astype(np.float64)
    return np.moveaxis((codes * scale).reshape(v.shape), -1, axis)


WIDE = False


def mx_kscale(k):
    if not WIDE:
        return np.ones(k)
    levels = np.array([30, -30])
    if k % 512:
        return np.exp2(np.random.permutation(np.resize(levels, k // 32))).repeat(32)
    a = np.empty((k // 512, 16))
    for p in range(k // 512):
        a[p, :8] = np.random.permutation(np.resize(levels, 8))
        for g in range(8):
            far = levels[np.abs(levels - a[p, g]) >= 10]
            a[p, g + 8] = far[np.random.randint(len(far))]
    return np.exp2(a.ravel()).repeat(32)


def f64(x):
    return np.asarray(x).astype(np.float64)


def striped(idx):
    return np.tile(np.asarray(idx).reshape(-1, 16).T, (8, 1)).astype(np.uint16)


def unstriped(offs):
    return offs[:16].T.reshape(-1).astype(np.int64)


E2M1 = np.array([0.0, 0.5, 1.0, 1.5, 2.0, 3.0, 4.0, 6.0, -0.0, -0.5, -1.0, -1.5, -2.0, -3.0, -4.0, -6.0])


def pack_weight(w, fmt):
    k, n = w.shape
    w = f64(np.asarray(w, np.float32).astype(ml_dtypes.bfloat16)).reshape(k // 32, 32, n)
    amax = np.abs(w).max(1)
    if fmt in ("e4m3", "e5m2"):
        byte = np.frexp(amax)[1] - 1 + 127 - (7 if fmt == "e4m3" else 14)
    else:
        mant, ex = np.frexp(amax / 6.0)
        byte = np.where(mant > 0.5, ex, ex - 1) + 127
    byte = np.clip(np.where(amax > 0, byte, 1), 1, 254)
    scaled = (w * np.exp2(127.0 - byte)[:, None, :]).reshape(k, n).astype(np.float32)
    by_word = np.ascontiguousarray(scaled.reshape(k // 512, 128, 4, n).transpose(0, 1, 3, 2))
    if fmt in ("e4m3", "e5m2"):
        words = by_word.astype(ml_dtypes.float8_e4m3fn if fmt == "e4m3" else ml_dtypes.float8_e5m2).view(np.uint8)
    else:
        c = by_word.astype(ml_dtypes.float4_e2m1fn).view(np.uint8) & 0xF
        words = (c[..., 0::2] | (c[..., 1::2] << 4)).reshape(k // 512, 128, 2 * n)
    return np.ascontiguousarray(words), np.ascontiguousarray(byte.astype(np.uint8).reshape(k // 512, 16, n))


def unpack_weight(words, scales, fmt):
    g, _, n = scales.shape
    words = np.ascontiguousarray(words).reshape(g, 128, n, -1)
    if fmt in ("e4m3", "e5m2"):
        vals = words.view(ml_dtypes.float8_e4m3fn if fmt == "e4m3" else ml_dtypes.float8_e5m2).astype(np.float64)
    else:
        nib = np.empty((g, 128, n, 4), np.uint8)
        nib[..., 0::2] = words & 0xF
        nib[..., 1::2] = words >> 4
        vals = E2M1[nib]
    vals = vals * np.repeat(np.exp2(scales.astype(np.float64) - 127.0), 8, axis=1)[..., None]
    return vals.transpose(0, 1, 3, 2).reshape(g * 512, n)


def sigmoid(v):
    return 1.0 / (1.0 + np.exp(-v))


def sgn(shape):
    return np.random.uniform(0.5, 2.0, shape) * np.where(np.random.standard_normal(shape) < 0, -1.0, 1.0)


K, T, J, R, F, Z, C, O, N, L, E = 512, 1024, 256, 512, 512, 1024, 512, 128, 256, 512, 1024


def setup_inputs():
    n = np.random.standard_normal
    idx = np.random.permutation(T)[:J]
    idx2 = np.random.permutation(Z)[:J]
    idx3 = np.random.permutation(C)[:J]
    idx4 = np.random.permutation(C)[:O]
    idx5 = np.random.permutation(C)[:O]
    idx6 = np.random.permutation(J)[:O]
    idx7 = np.random.permutation(E)[:O]
    ff = mx_kscale(F)
    fk = mx_kscale(K)
    fr = mx_kscale(R)
    fl = mx_kscale(L)
    xop = pack_weight(n((F, Z)) / ff[:, None], "e5m2")
    wp = pack_weight(n((K, R)) * 1 / np.sqrt(K) / fk[:, None], "e5m2")
    w2p = pack_weight(n((F, R)) * 1 / np.sqrt(F) * ff[:, None], "e4m3")
    wbp = pack_weight(n((R, N)) * 1 / np.sqrt(R) / fr[:, None], "e4m3")
    sxp = pack_weight(n((L, O)) / fl[:, None], "e5m2")
    wsp = pack_weight(n((L, N)) * 1 / np.sqrt(L) * fl[:, None], "e4m3")
    return {
        "xo_words": xop[0],
        "xo_scales": xop[1],
        "cq": (np.random.randint(-7, 8, (K, T)).astype(np.float64)).astype(np.float32),
        "gs": (np.random.uniform(0.1, 0.4, (K, 1)) * fk[:, None]).astype(np.float32),
        "w_words": wp[0],
        "w_scales": wp[1],
        "w2_words": w2p[0],
        "w2_scales": w2p[1],
        "sa": (np.random.uniform(0.5, 1.6, (R, 1)) * fr[:, None]).astype(np.float32),
        "sb": (np.random.uniform(0.5, 1.6, (R, 1)) * fr[:, None]).astype(np.float32),
        "sg": (sgn((R, 1))).astype(np.float32),
        "bg": (np.random.uniform(-2.0, 2.0, (R, 1))).astype(np.float32),
        "wb_words": wbp[0],
        "wb_scales": wbp[1],
        "sx_words": sxp[0],
        "sx_scales": sxp[1],
        "ws_words": wsp[0],
        "ws_scales": wsp[1],
        "offs": striped(idx),
        "offs2": striped(idx2),
        "offs3": striped(idx3),
        "offs4": striped(idx4),
        "offs5": striped(idx5),
        "offs6": striped(idx6),
        "offs7": striped(idx7),
    }


def reference(xo_words, xo_scales, cq, gs, w_words, w_scales, w2_words, w2_scales, sa, sb, sg, bg, wb_words, wb_scales, sx_words, sx_scales, ws_words, ws_scales, offs, offs2, offs3, offs4, offs5, offs6, offs7):
    idx = unstriped(offs)
    idx2 = unstriped(offs2)
    idx3 = unstriped(offs3)
    idx4 = unstriped(offs4)
    idx5 = unstriped(offs5)
    idx6 = unstriped(offs6)
    idx7 = unstriped(offs7)
    xou = unpack_weight(xo_words, xo_scales, "e5m2")
    wu = unpack_weight(w_words, w_scales, "e5m2")
    w2u = unpack_weight(w2_words, w2_scales, "e4m3")
    wbu = unpack_weight(wb_words, wb_scales, "e4m3")
    sxu = unpack_weight(sx_words, sx_scales, "e5m2")
    wsu = unpack_weight(ws_words, ws_scales, "e4m3")
    x1 = f64(cq)[:, idx] * f64(gs)
    x1q = mxq(x1, 0, "e4m3")
    a = wu.T @ x1q
    xoidx2g = xou[:, idx2]
    b = w2u.T @ xoidx2g
    pw = np.zeros((R, C))
    pw[:, idx3] = a
    hid = pw[:, idx4] * f64(sa) * sigmoid(pw[:, idx5] * f64(sg) + f64(bg)) - b[:, idx6] * f64(sb)
    hidq = mxq(hid, 0, "e5m2")
    p = wbu.T @ hidq + wsu.T @ sxu
    y = np.zeros((N, E))
    y[:, idx7] = p
    return y

@@ -1,0 +1,210 @@
+from contextlib import ExitStack
+
+import concourse.mybir as mybir
+
+K, T, J, R, F, Z, C, O, N, L, E = 512, 1024, 256, 512, 512, 1024, 512, 128, 256, 512, 1024
+FLOPS = 2 * (K * R * J + F * R * J + R * N * O + L * N * O)
+
+F32 = mybir.dt.float32
+BF16 = mybir.dt.bfloat16
+I32 = mybir.dt.int32
+U32 = mybir.dt.uint32
+U16 = mybir.dt.uint16
+U8 = mybir.dt.uint8
+E4M3 = mybir.dt.float8_e4m3fn_x4
+E5M2 = mybir.dt.float8_e5m2_x4
+ACT = mybir.ActivationFunctionType
+ALU = mybir.AluOpType
+
+P = 128
+PACK = 4
+QUADS = 4
+
+
+def tile_list_gatedreadless_codednote_further_scattered_kernel(
+    tc, xo_words, xo_scales, cq, gs, w_words, w_scales, w2_words, w2_scales, sa, sb, sg, bg,
+    wb_words, wb_scales, sx_words, sx_scales, ws_words, ws_scales,
+    offs, offs2, offs3, offs4, offs5, offs6, offs7, out,
+):
+    nc = tc.nc
+    with ExitStack() as ctx:
+        keep = ctx.enter_context(tc.tile_pool(name="keep", bufs=1))
+        psum = ctx.enter_context(tc.psum_pool(name="psum", bufs=1))
+
+        def tile(name, shape, dtype):
+            return keep.tile(shape, dtype, name=name, align_bytes=64)
+
+        def load_list(name, src):
+            dst = keep.tile(list(src.shape), U16, name=name)
+            nc.sync.dma_start(dst[:], src)
+            return dst
+
+        def load_words(name, src):
+            dst = tile(name, [P, src.shape[2]], U32)
+            nc.sync.dma_start(dst[:].bitcast(I32), src[0].rearrange("p n t -> p (n t)").bitcast(I32))
+            return dst
+
+        def load_factors(name, src, queue):
+            dst = tile(name, [P, PACK], F32)
+            queue.dma_start(dst[:], src.rearrange("(p t) o -> p (t o)", t=PACK))
+            return dst
+
+        def load_scale_rows(dst, src, queue):
+            queue.dma_start(dst.bitcast(I32), src[0].bitcast(I32).rearrange("(q r) c -> r q c", r=4))
+
+        def spread_scale_rows(plane, staged):
+            for q in range(QUADS):
+                nc.vector.tensor_copy(plane[32 * q : 32 * q + 4, :].bitcast(I32), staged[:, q, :].bitcast(I32))
+
+        xo_staged = tile("xo_staged", [4, QUADS, Z], U8)
+        w2_staged = tile("w2_staged", [4, QUADS, R], U8)
+        w_staged = tile("w_staged", [4, QUADS, R], U8)
+        late_staged = tile("late_staged", [4, QUADS, 2 * N + O], U8)
+        wb_cols, ws_cols, sx_cols = slice(0, N), slice(N, 2 * N), slice(2 * N, 2 * N + O)
+
+        cq_rows = cq.rearrange("(p t) c -> t p c", t=PACK)
+        cq_t = [tile("cq%d" % t, [P, T], F32) for t in range(PACK)]
+        idx2 = load_list("idx2", offs2)
+        load_scale_rows(xo_staged[:], xo_scales, nc.scalar)
+        load_scale_rows(w2_staged[:], w2_scales, nc.scalar)
+        xo_w = load_words("xo_w", xo_words)
+        w2_raw = load_words("w2_raw", w2_words)
+        gs_t = load_factors("gs_t", gs, nc.scalar)
+        idx = load_list("idx", offs)
+        nc.sync.dma_start(cq_t[0][:], cq_rows[0])
+        idx6 = load_list("idx6", offs6)
+        load_scale_rows(w_staged[:], w_scales, nc.scalar)
+        nc.sync.dma_start(cq_t[1][:], cq_rows[1])
+        sb_t = load_factors("sb_t", sb, nc.scalar)
+        nc.sync.dma_start(cq_t[2][:], cq_rows[2])
+        nc.sync.dma_start(cq_t[3][:], cq_rows[3])
+        w_raw = load_words("w_raw", w_words)
+        load_scale_rows(late_staged[:, :, wb_cols], wb_scales, nc.sync)
+        load_scale_rows(late_staged[:, :, ws_cols], ws_scales, nc.sync)
+        load_scale_rows(late_staged[:, :, sx_cols], sx_scales, nc.sync)
+        idx3 = load_list("idx3", offs3)
+        idx4 = load_list("idx4", offs4)
+        idx5 = load_list("idx5", offs5)
+        sa_t = load_factors("sa_t", sa, nc.sync)
+        sg_t = load_factors("sg_t", sg, nc.sync)
+        bg_t = load_factors("bg_t", bg, nc.sync)
+        ws_w = load_words("ws_w", ws_words)
+        sx_w = load_words("sx_w", sx_words)
+        wb_w = load_words("wb_w", wb_words)
+        idx7 = load_list("idx7", offs7)
+
+        xo_plane = tile("xo_plane", [P, Z], U8)
+        w2_plane_raw = tile("w2_plane_raw", [P, R], U8)
+        w_plane_raw = tile("w_plane_raw", [P, R], U8)
+        late_plane = tile("late_plane", [P, 2 * N + O], U8)
+        for plane in (xo_plane, w2_plane_raw, w_plane_raw, late_plane):
+            nc.vector.memset(plane[:].bitcast(I32), 0)
+        pw = [tile("pw%d" % t, [P, C], F32) for t in range(PACK)]
+        for t in range(PACK):
+            nc.vector.memset(pw[t][:], 0.0)
+        page = [tile("page%d" % h, [P, E], F32) for h in range(N // P)]
+        for h in range(N // P):
+            nc.vector.memset(page[h][:], 0.0)
+
+        def deal_words(name, raw):
+            dealt = tile(name, [P, R], U32)
+            nc.scalar.copy(dealt[:].rearrange("p (t m) -> p m t", t=PACK), raw[:].rearrange("p (m t) -> p m t", t=PACK))
+            return dealt
+
+        def deal_scales(name, plane_raw, staged):
+            spread_scale_rows(plane_raw, staged)
+            dealt = tile(name, [P, R], U8)
+            nc.vector.tensor_copy(dealt[:].rearrange("p (t m) -> p t m", t=PACK), plane_raw[:].rearrange("p (m t) -> p t m", t=PACK))
+            return dealt
+
+        x1_planes = tile("x1_planes", [P, PACK, J], BF16)
+        for t in range(PACK):
+            nc.scalar.activation(x1_planes[:, t, :], cq_t[t][:].indirect(idx[:]), ACT.Copy, scale=gs_t[:, t : t + 1])
+        w_w = deal_words("w_w", w_raw)
+        x1 = tile("x1", [P, J, PACK], BF16)
+        nc.vector.tensor_copy(
+            x1[:].rearrange("p (c i) t -> p c t i", i=4), x1_planes[:].rearrange("p t (c i) -> p c t i", i=4)
+        )
+        x1_w = tile("x1_w", [P, J], U32)
+        x1_s = tile("x1_s", [P, J], U8)
+        nc.vector.quantize_mx(out=x1_w[:].bitcast(E4M3), scales=x1_s[:], in_=x1[:].rearrange("p j t -> p (j t)"))
+
+        spread_scale_rows(xo_plane, xo_staged)
+        xg_w = tile("xg_w", [P, J], U32)
+        xg_s = tile("xg_s", [P, J], U8)
+        nc.vector.tensor_copy(xg_w[:], xo_w[:].indirect(idx2[:]))
+        nc.vector.tensor_copy(xg_s[:], xo_plane[:].indirect(idx2[:]))
+        w2_w = deal_words("w2_w", w2_raw)
+        w2_s = deal_scales("w2_s", w2_plane_raw, w2_staged)
+        w_s = deal_scales("w_s", w_plane_raw, w_staged)
+        b_ps = [psum.tile([P, 2, J], F32, name="b_ps%d" % u) for u in range(2)]
+        bb = tile("bb", [P, PACK, O], F32)
+        for t in range(PACK):
+            cols = slice(t * P, (t + 1) * P)
+            nc.tensor.matmul_mx(
+                out=b_ps[t // 2][:, t % 2, :], lhsT=w2_w[:, cols].bitcast(E4M3), lhsT_scale=w2_s[:, cols],
+                rhs=xg_w[:].bitcast(E5M2), rhs_scale=xg_s[:], start=True, stop=True,
+            )
+        for t in range(PACK):
+            b_sb = tile("b_sb%d" % t, [P, J], F32)
+            nc.vector.tensor_copy(b_sb[:], b_ps[t // 2][:, t % 2, :])
+            nc.scalar.activation(bb[:, t, :], b_sb[:].indirect(idx6[:]), ACT.Copy, scale=sb_t[:, t : t + 1])
+
+        a_ps = [psum.tile([P, J], F32, name="a_ps%d" % t) for t in range(PACK)]
+        for t in range(PACK):
+            cols = slice(t * P, (t + 1) * P)
+            nc.tensor.matmul_mx(
+                out=a_ps[t][:], lhsT=w_w[:, cols].bitcast(E5M2), lhsT_scale=w_s[:, cols],
+                rhs=x1_w[:].bitcast(E4M3), rhs_scale=x1_s[:], start=True, stop=True,
+            )
+        spread_scale_rows(late_plane, late_staged)
+        p_ps = [psum.tile([P, O], F32, name="p_ps%d" % h) for h in range(N // P)]
+        for h in range(N // P):
+            nc.tensor.matmul_mx(
+                out=p_ps[h][:], lhsT=ws_w[:, h * P : (h + 1) * P].bitcast(E4M3),
+                lhsT_scale=late_plane[:, N + h * P : N + (h + 1) * P],
+                rhs=sx_w[:].bitcast(E5M2), rhs_scale=late_plane[:, sx_cols], start=True, stop=False,
+            )
+
+        a_sb = [tile("a_sb%d" % t, [P, J], F32) for t in range(PACK)]
+        nc.vector.tensor_copy(a_sb[0][:], a_ps[0][:])
+        for t in range(1, PACK):
+            nc.scalar.copy(a_sb[t][:], a_ps[t][:])
+        for t in range(PACK - 1):
+            nc.vector.tensor_copy(pw[t][:].indirect(idx3[:]), a_sb[t][:])
+        nc.scalar.activation(pw[3][:].indirect(idx3[:]), a_sb[3][:], ACT.Copy)
+
+        prod = tile("prod", [P, PACK, O], F32)
+        for t in (0, 3, 1, 2):
+            looks = a_sb[3] if t == 0 else tile("looks%d" % t, [P, 2 * O], F32)
+            nc.scalar.activation(
+                looks[:, 0:O], pw[t][:].indirect(idx5[:]), ACT.Sigmoid,
+                bias=bg_t[:, t : t + 1], scale=sg_t[:, t : t + 1],
+            )
+            nc.scalar.activation(looks[:, O : 2 * O], pw[t][:].indirect(idx4[:]), ACT.Copy, scale=sa_t[:, t : t + 1])
+            nc.vector.tensor_tensor(prod[:, t, :], looks[:, 0:O], looks[:, O : 2 * O], ALU.mult)
+
+        hid = tile("hid", [P, O, PACK], BF16)
+        nc.vector.tensor_tensor(
+            hid[:].rearrange("p (c i) t -> p c t i", i=4),
+            prod[:].rearrange("p t (c i) -> p c t i", i=4),
+            bb[:].rearrange("p t (c i) -> p c t i", i=4),
+            ALU.subtract,
+        )
+        hid_w = tile("hid_w", [P, O], U32)
+        hid_s = tile("hid_s", [P, O], U8)
+        nc.vector.quantize_mx(out=hid_w[:].bitcast(E5M2), scales=hid_s[:], in_=hid[:].rearrange("p o t -> p (o t)"))
+
+        for h in range(N // P):
+            nc.tensor.matmul_mx(
+                out=p_ps[h][:], lhsT=wb_w[:, h * P : (h + 1) * P].bitcast(E4M3),
+                lhsT_scale=late_plane[:, h * P : (h + 1) * P],
+                rhs=hid_w[:].bitcast(E5M2), rhs_scale=hid_s[:], start=False, stop=True,
+            )
+        p_sb = [tile("p_sb%d" % h, [P, O], F32) for h in range(N // P)]
+        nc.vector.tensor_copy(p_sb[0][:], p_ps[0][:])
+        nc.vector.tensor_copy(page[0][:].indirect(idx7[:]), p_sb[0][:])
+        nc.sync.dma_start(out[0:P, :], page[0][:])
+        nc.scalar.copy(p_sb[1][:], p_ps[1][:])
+        nc.scalar.activation(page[1][:].indirect(idx7[:]), p_sb[1][:], ACT.Copy)
+        nc.scalar.dma_start(out[P : 2 * P, :], page[1][:])

@@ -19,6 +19,7 @@ ALU = mybir.AluOpType
 P = 128
 PACK = 4
 QUADS = 4
+SHARE = 128
 
 
 def tile_list_gatedreadless_codednote_further_scattered_kernel(
@@ -32,7 +33,7 @@ def tile_list_gatedreadless_codednote_further_scattered_kernel(
         psum = ctx.enter_context(tc.psum_pool(name="psum", bufs=1))
 
         def tile(name, shape, dtype):
-            return keep.tile(shape, dtype, name=name, align_bytes=64)
+            return keep.tile(shape, dtype, name=name, tag=name, align_bytes=64)
 
         def load_list(name, src):
             dst = keep.tile(list(src.shape), U16, name=name)
@@ -49,39 +50,40 @@ def tile_list_gatedreadless_codednote_further_scattered_kernel(
             queue.dma_start(dst[:], src.rearrange("(p t) o -> p (t o)", t=PACK))
             return dst
 
-        def load_scale_rows(dst, src, queue):
-            queue.dma_start(dst.bitcast(I32), src[0].bitcast(I32).rearrange("(q r) c -> r q c", r=4))
+        def load_scale_rows(staged, cols, src, queue):
+            for half in range(2):
+                queue.dma_start(
+                    staged[64 * half : 64 * half + 4, :, cols].bitcast(I32),
+                    src[0, 8 * half : 8 * half + 8, :].bitcast(I32).rearrange("(u r) c -> r u c", r=4),
+                )
 
         def spread_scale_rows(plane, staged):
             for q in range(QUADS):
-                nc.vector.tensor_copy(plane[32 * q : 32 * q + 4, :].bitcast(I32), staged[:, q, :].bitcast(I32))
+                half, u = divmod(q, 2)
+                nc.vector.tensor_copy(
+                    plane[32 * q : 32 * q + 4, :].bitcast(I32), staged[64 * half : 64 * half + 4, u, :].bitcast(I32)
+                )
 
-        xo_staged = tile("xo_staged", [4, QUADS, Z], U8)
-        w2_staged = tile("w2_staged", [4, QUADS, R], U8)
-        w_staged = tile("w_staged", [4, QUADS, R], U8)
-        late_staged = tile("late_staged", [4, QUADS, 2 * N + O], U8)
+        xo_staged = tile("xo_staged", [P, 2, Z], U8)
+        ww_staged = tile("ww_staged", [P, 2, 2 * R], U8)
         wb_cols, ws_cols, sx_cols = slice(0, N), slice(N, 2 * N), slice(2 * N, 2 * N + O)
 
         cq_rows = cq.rearrange("(p t) c -> t p c", t=PACK)
         cq_t = [tile("cq%d" % t, [P, T], F32) for t in range(PACK)]
         idx2 = load_list("idx2", offs2)
-        load_scale_rows(xo_staged[:], xo_scales, nc.scalar)
-        load_scale_rows(w2_staged[:], w2_scales, nc.scalar)
-        xo_w = load_words("xo_w", xo_words)
-        w2_raw = load_words("w2_raw", w2_words)
-        gs_t = load_factors("gs_t", gs, nc.scalar)
+        load_scale_rows(xo_staged, slice(0, Z), xo_scales, nc.scalar)
         idx = load_list("idx", offs)
+        xo_w = load_words("xo_w", xo_words)
+        load_scale_rows(ww_staged, slice(0, R), w2_scales, nc.scalar)
+        w2_raw = load_words("w2_raw", w2_words)
+        load_scale_rows(ww_staged, slice(R, 2 * R), w_scales, nc.sync)
         nc.sync.dma_start(cq_t[0][:], cq_rows[0])
-        idx6 = load_list("idx6", offs6)
-        load_scale_rows(w_staged[:], w_scales, nc.scalar)
-        nc.sync.dma_start(cq_t[1][:], cq_rows[1])
-        sb_t = load_factors("sb_t", sb, nc.scalar)
-        nc.sync.dma_start(cq_t[2][:], cq_rows[2])
-        nc.sync.dma_start(cq_t[3][:], cq_rows[3])
+        gs_t = load_factors("gs_t", gs, nc.sync)
+        for t in range(1, PACK):
+            nc.sync.dma_start(cq_t[t][:], cq_rows[t])
         w_raw = load_words("w_raw", w_words)
-        load_scale_rows(late_staged[:, :, wb_cols], wb_scales, nc.sync)
-        load_scale_rows(late_staged[:, :, ws_cols], ws_scales, nc.sync)
-        load_scale_rows(late_staged[:, :, sx_cols], sx_scales, nc.sync)
+        idx6 = load_list("idx6", offs6)
+        sb_t = load_factors("sb_t", sb, nc.sync)
         idx3 = load_list("idx3", offs3)
         idx4 = load_list("idx4", offs4)
         idx5 = load_list("idx5", offs5)
@@ -93,41 +95,47 @@ def tile_list_gatedreadless_codednote_further_scattered_kernel(
         wb_w = load_words("wb_w", wb_words)
         idx7 = load_list("idx7", offs7)
 
+        warm = tile("warm", [P, 1], F32)
+        warm_out = tile("warm_out", [P, 1], F32)
+        nc.gpsimd.memset(warm[:], 0.0)
+        nc.scalar.activation(warm_out[:], warm[:], ACT.Sigmoid)
         xo_plane = tile("xo_plane", [P, Z], U8)
-        w2_plane_raw = tile("w2_plane_raw", [P, R], U8)
-        w_plane_raw = tile("w_plane_raw", [P, R], U8)
+        ww_plane_raw = tile("ww_plane_raw", [P, 2 * R], U8)
         late_plane = tile("late_plane", [P, 2 * N + O], U8)
-        for plane in (xo_plane, w2_plane_raw, w_plane_raw, late_plane):
+        for plane in (xo_plane, ww_plane_raw, late_plane):
             nc.vector.memset(plane[:].bitcast(I32), 0)
-        pw = [tile("pw%d" % t, [P, C], F32) for t in range(PACK)]
-        for t in range(PACK):
-            nc.vector.memset(pw[t][:], 0.0)
-        page = [tile("page%d" % h, [P, E], F32) for h in range(N // P)]
-        for h in range(N // P):
-            nc.vector.memset(page[h][:], 0.0)
+        for src, cols in ((ws_scales, ws_cols), (sx_scales, sx_cols), (wb_scales, wb_cols)):
+            for q in range(QUADS):
+                nc.sync.dma_start(
+                    late_plane[32 * q : 32 * q + 4, cols].bitcast(I32), src[0, 4 * q : 4 * q + 4, :].bitcast(I32)
+                )
 
         def deal_words(name, raw):
             dealt = tile(name, [P, R], U32)
-            nc.scalar.copy(dealt[:].rearrange("p (t m) -> p m t", t=PACK), raw[:].rearrange("p (m t) -> p m t", t=PACK))
-            return dealt
-
-        def deal_scales(name, plane_raw, staged):
-            spread_scale_rows(plane_raw, staged)
-            dealt = tile(name, [P, R], U8)
-            nc.vector.tensor_copy(dealt[:].rearrange("p (t m) -> p t m", t=PACK), plane_raw[:].rearrange("p (m t) -> p t m", t=PACK))
+            nc.scalar.copy(
+                dealt[:].rearrange("p (t c i) -> p c t i", t=PACK, i=4),
+                raw[:].rearrange("p (c i t) -> p c t i", t=PACK, i=4),
+            )
             return dealt
 
         x1_planes = tile("x1_planes", [P, PACK, J], BF16)
         for t in range(PACK):
             nc.scalar.activation(x1_planes[:, t, :], cq_t[t][:].indirect(idx[:]), ACT.Copy, scale=gs_t[:, t : t + 1])
         w_w = deal_words("w_w", w_raw)
-        x1 = tile("x1", [P, J, PACK], BF16)
-        nc.vector.tensor_copy(
-            x1[:].rearrange("p (c i) t -> p c t i", i=4), x1_planes[:].rearrange("p t (c i) -> p c t i", i=4)
-        )
         x1_w = tile("x1_w", [P, J], U32)
         x1_s = tile("x1_s", [P, J], U8)
-        nc.vector.quantize_mx(out=x1_w[:].bitcast(E4M3), scales=x1_s[:], in_=x1[:].rearrange("p j t -> p (j t)"))
+        halves = [slice(0, J // 2), slice(J // 2, J)]
+        x1 = [tile("x1_%d" % u, [P, J // 2, PACK], BF16) for u in range(2)]
+        for pair in (slice(0, 2), slice(2, 4)):
+            for u, cols in enumerate(halves):
+                nc.vector.tensor_copy(
+                    x1[u][:, :, pair].rearrange("p (c i) t -> p c t i", i=4),
+                    x1_planes[:, pair, cols].rearrange("p t (c i) -> p c t i", i=4),
+                )
+        for u, cols in enumerate(halves):
+            nc.vector.quantize_mx(
+                out=x1_w[:, cols].bitcast(E4M3), scales=x1_s[:, cols], in_=x1[u][:].rearrange("p j t -> p (j t)")
+            )
 
         spread_scale_rows(xo_plane, xo_staged)
         xg_w = tile("xg_w", [P, J], U32)
@@ -135,10 +143,16 @@ def tile_list_gatedreadless_codednote_further_scattered_kernel(
         nc.vector.tensor_copy(xg_w[:], xo_w[:].indirect(idx2[:]))
         nc.vector.tensor_copy(xg_s[:], xo_plane[:].indirect(idx2[:]))
         w2_w = deal_words("w2_w", w2_raw)
-        w2_s = deal_scales("w2_s", w2_plane_raw, w2_staged)
-        w_s = deal_scales("w_s", w_plane_raw, w_staged)
+        spread_scale_rows(ww_plane_raw, ww_staged)
+        w2_s = tile("w2_s", [P, R], U8)
+        w_s = tile("w_s", [P, R], U8)
+        for u, dealt in enumerate((w2_s, w_s)):
+            nc.vector.tensor_copy(
+                dealt[:].rearrange("p (t m) -> p t m", t=PACK),
+                ww_plane_raw[:, u * R : (u + 1) * R].rearrange("p (m t) -> p t m", t=PACK),
+            )
         b_ps = [psum.tile([P, 2, J], F32, name="b_ps%d" % u) for u in range(2)]
-        bb = tile("bb", [P, PACK, O], F32)
+        bb = keep.tile([P, PACK, O], F32, name="bb", tag="w_raw", align_bytes=64)
         for t in range(PACK):
             cols = slice(t * P, (t + 1) * P)
             nc.tensor.matmul_mx(
@@ -146,19 +160,31 @@ def tile_list_gatedreadless_codednote_further_scattered_kernel(
                 rhs=xg_w[:].bitcast(E5M2), rhs_scale=xg_s[:], start=True, stop=True,
             )
         for t in range(PACK):
-            b_sb = tile("b_sb%d" % t, [P, J], F32)
+            b_tag = "b_sb%d" % t if t < 2 else "x1_%d" % (t - 2)
+            b_sb = keep.tile([P, J], F32, name="b_sb%d" % t, tag=b_tag, align_bytes=64)
             nc.vector.tensor_copy(b_sb[:], b_ps[t // 2][:, t % 2, :])
             nc.scalar.activation(bb[:, t, :], b_sb[:].indirect(idx6[:]), ACT.Copy, scale=sb_t[:, t : t + 1])
 
-        a_ps = [psum.tile([P, J], F32, name="a_ps%d" % t) for t in range(PACK)]
+        a_ps = [psum.tile([P, J], F32, name="a_ps%d" % t, tag="a_ps%d" % t) for t in range(PACK)]
         for t in range(PACK):
             cols = slice(t * P, (t + 1) * P)
             nc.tensor.matmul_mx(
                 out=a_ps[t][:], lhsT=w_w[:, cols].bitcast(E5M2), lhsT_scale=w_s[:, cols],
                 rhs=x1_w[:].bitcast(E4M3), rhs_scale=x1_s[:], start=True, stop=True,
             )
-        spread_scale_rows(late_plane, late_staged)
-        p_ps = [psum.tile([P, O], F32, name="p_ps%d" % h) for h in range(N // P)]
+        pw = [tile("pw%d" % t, [P, C], F32) for t in range(PACK)]
+        for t in range(PACK):
+            nc.gpsimd.memset(pw[t][:], 0.0)
+        page = [tile("page%d" % h, [P, E], F32) for h in range(N // P)]
+        for h in range(N // P):
+            nc.vector.memset(page[h][:], 0.0)
+        a_sb = [tile("a_sb%d" % t, [P, J], F32) for t in range(PACK)]
+        for t in range(PACK):
+            if t != 1:
+                nc.vector.tensor_copy(a_sb[t][:], a_ps[t][:])
+            else:
+                nc.scalar.copy(a_sb[t][:], a_ps[t][:])
+        p_ps = [psum.tile([P, O], F32, name="p_ps%d" % h, tag="a_ps%d" % h) for h in range(N // P)]
         for h in range(N // P):
             nc.tensor.matmul_mx(
                 out=p_ps[h][:], lhsT=ws_w[:, h * P : (h + 1) * P].bitcast(E4M3),
@@ -166,34 +192,41 @@ def tile_list_gatedreadless_codednote_further_scattered_kernel(
                 rhs=sx_w[:].bitcast(E5M2), rhs_scale=late_plane[:, sx_cols], start=True, stop=False,
             )
 
-        a_sb = [tile("a_sb%d" % t, [P, J], F32) for t in range(PACK)]
-        nc.vector.tensor_copy(a_sb[0][:], a_ps[0][:])
-        for t in range(1, PACK):
-            nc.scalar.copy(a_sb[t][:], a_ps[t][:])
-        for t in range(PACK - 1):
+        nc.vector.tensor_copy(pw[0][:].indirect(idx3[:, 0 : SHARE // 16]), a_sb[0][:, 0:SHARE])
+        nc.scalar.activation(pw[1][:].indirect(idx3[:]), a_sb[1][:], ACT.Copy)
+        nc.scalar.activation(pw[0][:].indirect(idx3[:, SHARE // 16 : J // 16]), a_sb[0][:, SHARE:J], ACT.Copy)
+        for t in (2, 3):
             nc.vector.tensor_copy(pw[t][:].indirect(idx3[:]), a_sb[t][:])
-        nc.scalar.activation(pw[3][:].indirect(idx3[:]), a_sb[3][:], ACT.Copy)
 
-        prod = tile("prod", [P, PACK, O], F32)
-        for t in (0, 3, 1, 2):
-            looks = a_sb[3] if t == 0 else tile("looks%d" % t, [P, 2 * O], F32)
+        gate = tile("gate", [P, PACK, O], F32)
+        read = tile("read", [P, PACK - 1, O], F32)
+        read_last = keep.tile([P, O], F32, name="read_last", tag="pw2", align_bytes=64)
+        for t in (1, 0, 2, 3):
             nc.scalar.activation(
-                looks[:, 0:O], pw[t][:].indirect(idx5[:]), ACT.Sigmoid,
+                gate[:, t, :], pw[t][:].indirect(idx5[:]), ACT.Sigmoid,
                 bias=bg_t[:, t : t + 1], scale=sg_t[:, t : t + 1],
             )
-            nc.scalar.activation(looks[:, O : 2 * O], pw[t][:].indirect(idx4[:]), ACT.Copy, scale=sa_t[:, t : t + 1])
-            nc.vector.tensor_tensor(prod[:, t, :], looks[:, 0:O], looks[:, O : 2 * O], ALU.mult)
+            dst = read[:, t, :] if t < PACK - 1 else read_last[:]
+            nc.scalar.activation(dst, pw[t][:].indirect(idx4[:]), ACT.Copy, scale=sa_t[:, t : t + 1])
+        prod = keep.tile([P, PACK, O], F32, name="prod", tag="a_sb3", align_bytes=64)
+        nc.vector.tensor_tensor(prod[:, 0 : PACK - 1, :], read[:], gate[:, 0 : PACK - 1, :], ALU.mult)
+        nc.vector.tensor_tensor(prod[:, PACK - 1, :], read_last[:], gate[:, PACK - 1, :], ALU.mult)
 
         hid = tile("hid", [P, O, PACK], BF16)
-        nc.vector.tensor_tensor(
-            hid[:].rearrange("p (c i) t -> p c t i", i=4),
-            prod[:].rearrange("p t (c i) -> p c t i", i=4),
-            bb[:].rearrange("p t (c i) -> p c t i", i=4),
-            ALU.subtract,
-        )
         hid_w = tile("hid_w", [P, O], U32)
         hid_s = tile("hid_s", [P, O], U8)
-        nc.vector.quantize_mx(out=hid_w[:].bitcast(E5M2), scales=hid_s[:], in_=hid[:].rearrange("p o t -> p (o t)"))
+        place_halves = [slice(0, O // 2), slice(O // 2, O)]
+        for cols in place_halves:
+            nc.vector.tensor_tensor(
+                hid[:, cols, :].rearrange("p (c i) t -> p c t i", i=4),
+                prod[:, :, cols].rearrange("p t (c i) -> p c t i", i=4),
+                bb[:, :, cols].rearrange("p t (c i) -> p c t i", i=4),
+                ALU.subtract,
+            )
+        for cols in place_halves:
+            nc.vector.quantize_mx(
+                out=hid_w[:, cols].bitcast(E5M2), scales=hid_s[:, cols], in_=hid[:, cols, :].rearrange("p o t -> p (o t)")
+            )
 
         for h in range(N // P):
             nc.tensor.matmul_mx(

from contextlib import ExitStack

import concourse.mybir as mybir

K, T, J, R, F, Z, C, O, N, L, E = 512, 1024, 256, 512, 512, 1024, 512, 128, 256, 512, 1024
FLOPS = 2 * (K * R * J + F * R * J + R * N * O + L * N * O)

F32 = mybir.dt.float32
BF16 = mybir.dt.bfloat16
I32 = mybir.dt.int32
U32 = mybir.dt.uint32
U16 = mybir.dt.uint16
U8 = mybir.dt.uint8
E4M3 = mybir.dt.float8_e4m3fn_x4
E5M2 = mybir.dt.float8_e5m2_x4
ACT = mybir.ActivationFunctionType
ALU = mybir.AluOpType

P = 128
PACK = 4
QUADS = 4
SHARE = 128


def tile_list_gatedreadless_codednote_further_scattered_kernel(
    tc, xo_words, xo_scales, cq, gs, w_words, w_scales, w2_words, w2_scales, sa, sb, sg, bg,
    wb_words, wb_scales, sx_words, sx_scales, ws_words, ws_scales,
    offs, offs2, offs3, offs4, offs5, offs6, offs7, out,
):
    nc = tc.nc
    with ExitStack() as ctx:
        keep = ctx.enter_context(tc.tile_pool(name="keep", bufs=1))
        psum = ctx.enter_context(tc.psum_pool(name="psum", bufs=1))

        def tile(name, shape, dtype):
            return keep.tile(shape, dtype, name=name, tag=name, align_bytes=64)

        def load_list(name, src):
            dst = keep.tile(list(src.shape), U16, name=name)
            nc.sync.dma_start(dst[:], src)
            return dst

        def load_words(name, src):
            dst = tile(name, [P, src.shape[2]], U32)
            nc.sync.dma_start(dst[:].bitcast(I32), src[0].rearrange("p n t -> p (n t)").bitcast(I32))
            return dst

        def load_factors(name, src, queue):
            dst = tile(name, [P, PACK], F32)
            queue.dma_start(dst[:], src.rearrange("(p t) o -> p (t o)", t=PACK))
            return dst

        def load_scale_rows(staged, cols, src, queue):
            for half in range(2):
                queue.dma_start(
                    staged[64 * half : 64 * half + 4, :, cols].bitcast(I32),
                    src[0, 8 * half : 8 * half + 8, :].bitcast(I32).rearrange("(u r) c -> r u c", r=4),
                )

        def spread_scale_rows(plane, staged):
            for q in range(QUADS):
                half, u = divmod(q, 2)
                nc.vector.tensor_copy(
                    plane[32 * q : 32 * q + 4, :].bitcast(I32), staged[64 * half : 64 * half + 4, u, :].bitcast(I32)
                )

        xo_staged = tile("xo_staged", [P, 2, Z], U8)
        ww_staged = tile("ww_staged", [P, 2, 2 * R], U8)
        wb_cols, ws_cols, sx_cols = slice(0, N), slice(N, 2 * N), slice(2 * N, 2 * N + O)

        cq_rows = cq.rearrange("(p t) c -> t p c", t=PACK)
        cq_t = [tile("cq%d" % t, [P, T], F32) for t in range(PACK)]
        idx2 = load_list("idx2", offs2)
        load_scale_rows(xo_staged, slice(0, Z), xo_scales, nc.scalar)
        idx = load_list("idx", offs)
        xo_w = load_words("xo_w", xo_words)
        load_scale_rows(ww_staged, slice(0, R), w2_scales, nc.scalar)
        w2_raw = load_words("w2_raw", w2_words)
        load_scale_rows(ww_staged, slice(R, 2 * R), w_scales, nc.sync)
        nc.sync.dma_start(cq_t[0][:], cq_rows[0])
        gs_t = load_factors("gs_t", gs, nc.sync)
        for t in range(1, PACK):
            nc.sync.dma_start(cq_t[t][:], cq_rows[t])
        w_raw = load_words("w_raw", w_words)
        idx6 = load_list("idx6", offs6)
        sb_t = load_factors("sb_t", sb, nc.sync)
        idx3 = load_list("idx3", offs3)
        idx4 = load_list("idx4", offs4)
        idx5 = load_list("idx5", offs5)
        sa_t = load_factors("sa_t", sa, nc.sync)
        sg_t = load_factors("sg_t", sg, nc.sync)
        bg_t = load_factors("bg_t", bg, nc.sync)
        ws_w = load_words("ws_w", ws_words)
        sx_w = load_words("sx_w", sx_words)
        wb_w = load_words("wb_w", wb_words)
        idx7 = load_list("idx7", offs7)

        warm = tile("warm", [P, 1], F32)
        warm_out = tile("warm_out", [P, 1], F32)
        nc.gpsimd.memset(warm[:], 0.0)
        nc.scalar.activation(warm_out[:], warm[:], ACT.Sigmoid)
        xo_plane = tile("xo_plane", [P, Z], U8)
        ww_plane_raw = tile("ww_plane_raw", [P, 2 * R], U8)
        late_plane = tile("late_plane", [P, 2 * N + O], U8)
        for plane in (xo_plane, ww_plane_raw, late_plane):
            nc.vector.memset(plane[:].bitcast(I32), 0)
        for src, cols in ((ws_scales, ws_cols), (sx_scales, sx_cols), (wb_scales, wb_cols)):
            for q in range(QUADS):
                nc.sync.dma_start(
                    late_plane[32 * q : 32 * q + 4, cols].bitcast(I32), src[0, 4 * q : 4 * q + 4, :].bitcast(I32)
                )

        def deal_words(name, raw):
            dealt = tile(name, [P, R], U32)
            nc.scalar.copy(
                dealt[:].rearrange("p (t c i) -> p c t i", t=PACK, i=4),
                raw[:].rearrange("p (c i t) -> p c t i", t=PACK, i=4),
            )
            return dealt

        x1_planes = tile("x1_planes", [P, PACK, J], BF16)
        for t in range(PACK):
            nc.scalar.activation(x1_planes[:, t, :], cq_t[t][:].indirect(idx[:]), ACT.Copy, scale=gs_t[:, t : t + 1])
        w_w = deal_words("w_w", w_raw)
        x1_w = tile("x1_w", [P, J], U32)
        x1_s = tile("x1_s", [P, J], U8)
        halves = [slice(0, J // 2), slice(J // 2, J)]
        x1 = [tile("x1_%d" % u, [P, J // 2, PACK], BF16) for u in range(2)]
        for pair in (slice(0, 2), slice(2, 4)):
            for u, cols in enumerate(halves):
                nc.vector.tensor_copy(
                    x1[u][:, :, pair].rearrange("p (c i) t -> p c t i", i=4),
                    x1_planes[:, pair, cols].rearrange("p t (c i) -> p c t i", i=4),
                )
        for u, cols in enumerate(halves):
            nc.vector.quantize_mx(
                out=x1_w[:, cols].bitcast(E4M3), scales=x1_s[:, cols], in_=x1[u][:].rearrange("p j t -> p (j t)")
            )

        spread_scale_rows(xo_plane, xo_staged)
        xg_w = tile("xg_w", [P, J], U32)
        xg_s = tile("xg_s", [P, J], U8)
        nc.vector.tensor_copy(xg_w[:], xo_w[:].indirect(idx2[:]))
        nc.vector.tensor_copy(xg_s[:], xo_plane[:].indirect(idx2[:]))
        w2_w = deal_words("w2_w", w2_raw)
        spread_scale_rows(ww_plane_raw, ww_staged)
        w2_s = tile("w2_s", [P, R], U8)
        w_s = tile("w_s", [P, R], U8)
        for u, dealt in enumerate((w2_s, w_s)):
            nc.vector.tensor_copy(
                dealt[:].rearrange("p (t m) -> p t m", t=PACK),
                ww_plane_raw[:, u * R : (u + 1) * R].rearrange("p (m t) -> p t m", t=PACK),
            )
        b_ps = [psum.tile([P, 2, J], F32, name="b_ps%d" % u) for u in range(2)]
        bb = keep.tile([P, PACK, O], F32, name="bb", tag="w_raw", align_bytes=64)
        for t in range(PACK):
            cols = slice(t * P, (t + 1) * P)
            nc.tensor.matmul_mx(
                out=b_ps[t // 2][:, t % 2, :], lhsT=w2_w[:, cols].bitcast(E4M3), lhsT_scale=w2_s[:, cols],
                rhs=xg_w[:].bitcast(E5M2), rhs_scale=xg_s[:], start=True, stop=True,
            )
        for t in range(PACK):
            b_tag = "b_sb%d" % t if t < 2 else "x1_%d" % (t - 2)
            b_sb = keep.tile([P, J], F32, name="b_sb%d" % t, tag=b_tag, align_bytes=64)
            nc.vector.tensor_copy(b_sb[:], b_ps[t // 2][:, t % 2, :])
            nc.scalar.activation(bb[:, t, :], b_sb[:].indirect(idx6[:]), ACT.Copy, scale=sb_t[:, t : t + 1])

        a_ps = [psum.tile([P, J], F32, name="a_ps%d" % t, tag="a_ps%d" % t) for t in range(PACK)]
        for t in range(PACK):
            cols = slice(t * P, (t + 1) * P)
            nc.tensor.matmul_mx(
                out=a_ps[t][:], lhsT=w_w[:, cols].bitcast(E5M2), lhsT_scale=w_s[:, cols],
                rhs=x1_w[:].bitcast(E4M3), rhs_scale=x1_s[:], start=True, stop=True,
            )
        pw = [tile("pw%d" % t, [P, C], F32) for t in range(PACK)]
        for t in range(PACK):
            nc.gpsimd.memset(pw[t][:], 0.0)
        page = [tile("page%d" % h, [P, E], F32) for h in range(N // P)]
        for h in range(N // P):
            nc.vector.memset(page[h][:], 0.0)
        a_sb = [tile("a_sb%d" % t, [P, J], F32) for t in range(PACK)]
        for t in range(PACK):
            if t != 1:
                nc.vector.tensor_copy(a_sb[t][:], a_ps[t][:])
            else:
                nc.scalar.copy(a_sb[t][:], a_ps[t][:])
        p_ps = [psum.tile([P, O], F32, name="p_ps%d" % h, tag="a_ps%d" % h) for h in range(N // P)]
        for h in range(N // P):
            nc.tensor.matmul_mx(
                out=p_ps[h][:], lhsT=ws_w[:, h * P : (h + 1) * P].bitcast(E4M3),
                lhsT_scale=late_plane[:, N + h * P : N + (h + 1) * P],
                rhs=sx_w[:].bitcast(E5M2), rhs_scale=late_plane[:, sx_cols], start=True, stop=False,
            )

        nc.vector.tensor_copy(pw[0][:].indirect(idx3[:, 0 : SHARE // 16]), a_sb[0][:, 0:SHARE])
        nc.scalar.activation(pw[1][:].indirect(idx3[:]), a_sb[1][:], ACT.Copy)
        nc.scalar.activation(pw[0][:].indirect(idx3[:, SHARE // 16 : J // 16]), a_sb[0][:, SHARE:J], ACT.Copy)
        for t in (2, 3):
            nc.vector.tensor_copy(pw[t][:].indirect(idx3[:]), a_sb[t][:])

        gate = tile("gate", [P, PACK, O], F32)
        read = tile("read", [P, PACK - 1, O], F32)
        read_last = keep.tile([P, O], F32, name="read_last", tag="pw2", align_bytes=64)
        for t in (1, 0, 2, 3):
            nc.scalar.activation(
                gate[:, t, :], pw[t][:].indirect(idx5[:]), ACT.Sigmoid,
                bias=bg_t[:, t : t + 1], scale=sg_t[:, t : t + 1],
            )
            dst = read[:, t, :] if t < PACK - 1 else read_last[:]
            nc.scalar.activation(dst, pw[t][:].indirect(idx4[:]), ACT.Copy, scale=sa_t[:, t : t + 1])
        prod = keep.tile([P, PACK, O], F32, name="prod", tag="a_sb3", align_bytes=64)
        nc.vector.tensor_tensor(prod[:, 0 : PACK - 1, :], read[:], gate[:, 0 : PACK - 1, :], ALU.mult)
        nc.vector.tensor_tensor(prod[:, PACK - 1, :], read_last[:], gate[:, PACK - 1, :], ALU.mult)

        hid = tile("hid", [P, O, PACK], BF16)
        hid_w = tile("hid_w", [P, O], U32)
        hid_s = tile("hid_s", [P, O], U8)
        place_halves = [slice(0, O // 2), slice(O // 2, O)]
        for cols in place_halves:
            nc.vector.tensor_tensor(
                hid[:, cols, :].rearrange("p (c i) t -> p c t i", i=4),
                prod[:, :, cols].rearrange("p t (c i) -> p c t i", i=4),
                bb[:, :, cols].rearrange("p t (c i) -> p c t i", i=4),
                ALU.subtract,
            )
        for cols in place_halves:
            nc.vector.quantize_mx(
                out=hid_w[:, cols].bitcast(E5M2), scales=hid_s[:, cols], in_=hid[:, cols, :].rearrange("p o t -> p (o t)")
            )

        for h in range(N // P):
            nc.tensor.matmul_mx(
                out=p_ps[h][:], lhsT=wb_w[:, h * P : (h + 1) * P].bitcast(E4M3),
                lhsT_scale=late_plane[:, h * P : (h + 1) * P],
                rhs=hid_w[:].bitcast(E5M2), rhs_scale=hid_s[:], start=False, stop=True,
            )
        p_sb = [tile("p_sb%d" % h, [P, O], F32) for h in range(N // P)]
        nc.vector.tensor_copy(p_sb[0][:], p_ps[0][:])
        nc.vector.tensor_copy(page[0][:].indirect(idx7[:]), p_sb[0][:])
        nc.sync.dma_start(out[0:P, :], page[0][:])
        nc.scalar.copy(p_sb[1][:], p_ps[1][:])
        nc.scalar.activation(page[1][:].indirect(idx7[:]), p_sb[1][:], ACT.Copy)
        nc.scalar.dma_start(out[P : 2 * P, :], page[1][:])
